import numpy as np, ml_dtypes
CORES = [40,64,80,88,96,104,120,144]
N = 8
KT, HT, TK = 4, 1, 128
def setup_inputs(rng):
    w = (rng.standard_normal((128, KT * HT * 128), dtype=np.float32) / 8).astype(ml_dtypes.bfloat16)
    return {"x": rng.standard_normal((N, 128, KT * TK), dtype=np.float32).astype(ml_dtypes.bfloat16), "w": np.broadcast_to(w, (N,) + w.shape).copy()}
def setup_inputs_big(rng):
    d = setup_inputs(rng)
    for k in ("x", "w"): d[k] = (d[k].astype(np.float32) * 1024.0).astype(d[k].dtype)
    return d
def setup_inputs_small(rng):
    d = setup_inputs(rng)
    for k in ("x", "w"): d[k] = (d[k].astype(np.float32) * (1 / 1024.0)).astype(d[k].dtype)
    return d
def setup_inputs_apart(rng):
    d = setup_inputs(rng)
    f = (10.0 ** rng.permutation(np.linspace(-1.5, 1.5, N))).astype(np.float32).reshape(N, 1, 1)
    for k in ("x",): d[k] = (d[k].astype(np.float32) * f).astype(d[k].dtype)
    return d
def tie_inputs(x):
    x = dict(x)
    x["w"] = np.broadcast_to(x["w"][0], x["w"].shape).copy()
    return x
def reference(x, w):
    X, W = x.astype(np.float64), w.astype(np.float64)
    def hidden(r):
        return np.stack([np.maximum(sum(W[r][:, 128 * (HT * t + u):128 * (HT * t + u) + 128].T @ X[r][:, TK * t:TK * t + TK] for t in range(KT)), 0.0) for u in range(HT)])
    h = [hidden(r) for r in range(N)]
    y = np.stack([sum(h[(r - 1) % N][u].T @ h[r][u] for u in range(HT)) for r in range(N)])
    return {"y": y.astype(ml_dtypes.bfloat16 if x.dtype != np.float64 else np.float64)}

@@ -1,0 +1,92 @@
+from concourse.mybir import AluOpType
+
+SIM_CORES = 256
+TK = 128
+KT = 4
+ENG_CHIP = 8
+ENG_OUT = 8
+
+SCRATCH = {
+    "xs": ("sbuf", [128, KT * TK], "bfloat16"),
+    "ws": ("sbuf", [128, KT * TK], "bfloat16"),
+    "zero": ("sbuf", [128, TK], "float32"),
+    "h": ("sbuf", [128, TK], "bfloat16"),
+    "hp": ("sbuf", [128, TK], "bfloat16"),
+    "ys": ("sbuf", [128, TK], "bfloat16"),
+    "ps1": ("psum", [128, 512], "float32"),
+    "ps2": ("psum", [128, 512], "float32"),
+}
+SEMAPHORES = ["ld", "zs", "mm1", "hs", "arr", "snt", "mm2", "yr", "st"]
+
+
+def _same_chip(topo, a, b):
+    return topo.host(a) == topo.host(b) and topo.chip(a) == topo.chip(b)
+
+
+def _engines(topo, src, dst):
+    allowed = topo.mask(src, dst)
+    bits = [b for b in range(allowed.bit_length()) if (allowed >> b) & 1]
+    n = min(ENG_CHIP if _same_chip(topo, src, dst) else ENG_OUT, len(bits))
+    m = 0
+    for b in bits[::len(bits) // n][:n]:
+        m |= 1 << b
+    return m, n
+
+
+def _way(topo, T, src, dst):
+    if topo.may_write(src, dst):
+        return [src, dst]
+    c = [k for k in range(SIM_CORES)
+         if k != src and T.rank_of(k) is None and _same_chip(topo, k, src) and topo.may_write(k, dst)]
+    c.sort(key=lambda k: (topo.die(k) != topo.die(src), k))
+    return [src, c[0], dst]
+
+
+def _send(g, T, topo, core, dst, src_ap):
+    m, n = _engines(topo, core, dst)
+    rid, pid = topo.addr(dst, core)
+    g.remote_dma(T.hp[:], src_ap, T.sem.arr, T.sem.snt, pid, rid, m)
+    return n
+
+
+def rank_program(g, core, T, topo):
+    cores = list(T.cores)
+    n_ranks = len(cores)
+    ways = [_way(topo, T, cores[r], cores[(r + 1) % n_ranks]) for r in range(n_ranks)]
+    rank = T.rank_of(core)
+
+    if rank is None:
+        for w in ways:
+            if len(w) == 3 and w[1] == core:
+                g.wait_ge(T.sem.arr, _engines(topo, w[0], core)[1])
+                n = _send(g, T, topo, core, w[2], T.hp[:])
+                g.wait_ge(T.sem.snt, n)
+        return
+
+    s = T.sem
+    g.sync.dma_start(T.xs[:], T.x[:]).then_inc(s.ld, 16)
+    g.scalar.dma_start(T.ws[:], T.w[:]).then_inc(s.ld, 16)
+    g.vector.memset(T.zero[:], 0.0).then_inc(s.zs, 1)
+
+    g.tensor.wait_ge(s.ld, 32)
+    for t in range(KT):
+        mm = g.tensor.matmul(T.ps1[:, 0:TK], T.ws[:, t * TK:(t + 1) * TK], T.xs[:, t * TK:(t + 1) * TK],
+                             start=(t == 0), stop=(t == KT - 1))
+    mm.then_inc(s.mm1, 1)
+    g.vector.wait_ge(s.zs, 1)
+    g.vector.wait_ge(s.mm1, 1)
+    g.vector.tensor_tensor(T.h[:], T.ps1[:, 0:TK], T.zero[:], AluOpType.max).then_inc(s.hs, 1)
+
+    g.wait_ge(s.hs, 1)
+    n_out = _send(g, T, topo, core, ways[rank][1], T.h[:])
+
+    win = ways[(rank - 1) % n_ranks]
+    g.tensor.wait_ge(s.hs, 1)
+    g.tensor.wait_ge(s.arr, _engines(topo, win[-2], core)[1])
+    g.tensor.matmul(T.ps2[:, 0:TK], T.hp[:], T.h[:], start=True, stop=True).then_inc(s.mm2, 1)
+    g.vector.wait_ge(s.mm2, 1)
+    g.vector.tensor_copy(T.ys[:], T.ps2[:, 0:TK]).then_inc(s.yr, 1)
+    g.sync.wait_ge(s.yr, 1)
+    g.sync.dma_start(T.y[:], T.ys[:]).then_inc(s.st, 16)
+    g.sync.wait_ge(s.st, 16)
+    g.wait_ge(s.snt, n_out)

@@ -10,13 +10,19 @@ SCRATCH = {
     "xs": ("sbuf", [128, KT * TK], "bfloat16"),
     "ws": ("sbuf", [128, KT * TK], "bfloat16"),
     "zero": ("sbuf", [128, TK], "float32"),
+    "n1": ("sbuf", [128, TK], "bfloat16"),
     "h": ("sbuf", [128, TK], "bfloat16"),
-    "hp": ("sbuf", [128, TK], "bfloat16"),
+    "hn": ("sbuf", [128, TK], "bfloat16"),
+    "xe": ("sbuf", [128, TK], "bfloat16"),
+    "nl": ("sbuf", [128, TK], "bfloat16"),
+    "m": ("sbuf", [128, TK], "bfloat16"),
     "ys": ("sbuf", [128, TK], "bfloat16"),
-    "ps1": ("psum", [128, 512], "float32"),
-    "ps2": ("psum", [128, 512], "float32"),
+    "psa": ("psum", [128, 512], "float32"),
+    "psh": ("psum", [128, 512], "float32"),
+    "psq": ("psum", [128, 512], "float32"),
+    "psy": ("psum", [128, 512], "float32"),
 }
-SEMAPHORES = ["ld", "zs", "mm1", "hs", "arr", "snt", "mm2", "yr", "st"]
+SEMAPHORES = ["le", "lx", "lw", "zs", "sa", "sn", "sh", "shr", "shn", "ae", "al", "sq", "sm", "snt", "sy", "yr", "st"]
 
 
 def _same_chip(topo, a, b):
@@ -42,10 +48,10 @@ def _way(topo, T, src, dst):
     return [src, c[0], dst]
 
 
-def _send(g, T, topo, core, dst, src_ap):
+def _send(g, T, topo, core, dst, out_ap, src_ap, sem):
     m, n = _engines(topo, core, dst)
     rid, pid = topo.addr(dst, core)
-    g.remote_dma(T.hp[:], src_ap, T.sem.arr, T.sem.snt, pid, rid, m)
+    g.remote_dma(out_ap, src_ap, sem, T.sem.snt, pid, rid, m)
     return n
 
 
@@ -54,38 +60,72 @@ def rank_program(g, core, T, topo):
     n_ranks = len(cores)
     ways = [_way(topo, T, cores[r], cores[(r + 1) % n_ranks]) for r in range(n_ranks)]
     rank = T.rank_of(core)
+    s = T.sem
 
     if rank is None:
         for w in ways:
             if len(w) == 3 and w[1] == core:
-                g.wait_ge(T.sem.arr, _engines(topo, w[0], core)[1])
-                n = _send(g, T, topo, core, w[2], T.hp[:])
-                g.wait_ge(T.sem.snt, n)
+                n_in = _engines(topo, w[0], core)[1]
+                g.wait_ge(s.ae, n_in)
+                n = _send(g, T, topo, core, w[2], T.xe[:], T.xe[:], s.ae)
+                g.wait_ge(s.al, n_in)
+                n += _send(g, T, topo, core, w[2], T.nl[:], T.nl[:], s.al)
+                g.wait_ge(s.snt, n)
         return
 
-    s = T.sem
-    g.sync.dma_start(T.xs[:], T.x[:]).then_inc(s.ld, 16)
-    g.scalar.dma_start(T.ws[:], T.w[:]).then_inc(s.ld, 16)
+    def tile(buf, t):
+        return buf[:, t * TK:(t + 1) * TK]
+
+    last = KT - 1
+    cut = last * TK
+    nxt = ways[rank][1]
+    n_in = _engines(topo, ways[(rank - 1) % n_ranks][-2], core)[1]
+
+    for q, lo, hi in ((g.sync, 0, 64), (g.scalar, 64, 128)):
+        q.dma_start(T.xs[lo:hi, cut:], T.x[lo:hi, cut:]).then_inc(s.le, 16)
+    for q, lo, hi in ((g.sync, 0, 64), (g.scalar, 64, 128)):
+        q.dma_start(T.xs[lo:hi, 0:cut], T.x[lo:hi, 0:cut]).then_inc(s.lx, 16)
+    for q, lo, hi in ((g.sync, 0, 64), (g.scalar, 64, 128)):
+        q.dma_start(T.ws[lo:hi, :], T.w[lo:hi, :]).then_inc(s.lw, 16)
     g.vector.memset(T.zero[:], 0.0).then_inc(s.zs, 1)
 
-    g.tensor.wait_ge(s.ld, 32)
-    for t in range(KT):
-        mm = g.tensor.matmul(T.ps1[:, 0:TK], T.ws[:, t * TK:(t + 1) * TK], T.xs[:, t * TK:(t + 1) * TK],
-                             start=(t == 0), stop=(t == KT - 1))
-    mm.then_inc(s.mm1, 1)
+    g.wait_ge(s.le, 32)
+    n_out = _send(g, T, topo, core, nxt, T.xe[:], tile(T.xs, last), s.ae)
+
+    g.tensor.wait_ge(s.le, 32)
+    g.tensor.wait_ge(s.lx, 32)
+    g.tensor.wait_ge(s.lw, 32)
+    for t in range(last):
+        mm = g.tensor.matmul(T.psa[:, 0:TK], tile(T.ws, t), tile(T.xs, t), start=(t == 0), stop=(t == last - 1))
+    mm.then_inc(s.sa, 1)
     g.vector.wait_ge(s.zs, 1)
-    g.vector.wait_ge(s.mm1, 1)
-    g.vector.tensor_tensor(T.h[:], T.ps1[:, 0:TK], T.zero[:], AluOpType.max).then_inc(s.hs, 1)
+    g.vector.wait_ge(s.sa, 1)
+    g.vector.tensor_tensor(T.n1[:], T.zero[:], T.psa[:, 0:TK], AluOpType.subtract).then_inc(s.sn, 1)
+    g.wait_ge(s.sn, 1)
+    n_out += _send(g, T, topo, core, nxt, T.nl[:], T.n1[:], s.al)
 
-    g.wait_ge(s.hs, 1)
-    n_out = _send(g, T, topo, core, ways[rank][1], T.h[:])
+    for t in range(KT):
+        mm = g.tensor.matmul(T.psh[:, 0:TK], tile(T.ws, t), tile(T.xs, t), start=(t == 0), stop=(t == last))
+    mm.then_inc(s.sh, 1)
+    g.vector.wait_ge(s.sh, 1)
+    g.vector.tensor_tensor(T.h[:], T.psh[:, 0:TK], T.zero[:], AluOpType.max).then_inc(s.shr, 1)
+    g.vector.wait_ge(s.shr, 1)
+    g.vector.tensor_tensor(T.hn[:], T.zero[:], T.h[:], AluOpType.subtract).then_inc(s.shn, 1)
 
-    win = ways[(rank - 1) % n_ranks]
-    g.tensor.wait_ge(s.hs, 1)
-    g.tensor.wait_ge(s.arr, _engines(topo, win[-2], core)[1])
-    g.tensor.matmul(T.ps2[:, 0:TK], T.hp[:], T.h[:], start=True, stop=True).then_inc(s.mm2, 1)
-    g.vector.wait_ge(s.mm2, 1)
-    g.vector.tensor_copy(T.ys[:], T.ps2[:, 0:TK]).then_inc(s.yr, 1)
+    g.tensor.wait_ge(s.ae, n_in)
+    g.tensor.matmul(T.psq[:, 0:TK], tile(T.ws, last), T.xe[:], start=True, stop=True).then_inc(s.sq, 1)
+
+    g.tensor.wait_ge(s.shr, 1)
+    g.tensor.wait_ge(s.shn, 1)
+    g.tensor.wait_ge(s.al, n_in)
+    g.tensor.matmul(T.psy[:, 0:TK], T.nl[:], T.hn[:], start=True, stop=False)
+    g.vector.wait_ge(s.sq, 1)
+    g.vector.wait_ge(s.al, n_in)
+    g.vector.tensor_tensor(T.m[:], T.psq[:, 0:TK], T.nl[:], AluOpType.max).then_inc(s.sm, 1)
+    g.tensor.wait_ge(s.sm, 1)
+    g.tensor.matmul(T.psy[:, 0:TK], T.m[:], T.h[:], start=False, stop=True).then_inc(s.sy, 1)
+    g.vector.wait_ge(s.sy, 1)
+    g.vector.tensor_copy(T.ys[:], T.psy[:, 0:TK]).then_inc(s.yr, 1)
     g.sync.wait_ge(s.yr, 1)
     g.sync.dma_start(T.y[:], T.ys[:]).then_inc(s.st, 16)
     g.sync.wait_ge(s.st, 16)

@@ -3,17 +3,22 @@ from concourse.mybir import AluOpType
 SIM_CORES = 256
 TK = 128
 KT = 4
+CUT = 112
+WD = (128 - CUT) * KT * TK // 128
+G = TK // WD
 ENG_CHIP = 8
 ENG_OUT = 8
 
 SCRATCH = {
     "xs": ("sbuf", [128, KT * TK], "bfloat16"),
     "ws": ("sbuf", [128, KT * TK], "bfloat16"),
+    "wq": ("sbuf", [128, G * TK], "bfloat16"),
+    "xd": ("dram", [128, WD], "bfloat16"),
     "zero": ("sbuf", [128, TK], "float32"),
     "n1": ("sbuf", [128, TK], "bfloat16"),
     "h": ("sbuf", [128, TK], "bfloat16"),
     "hn": ("sbuf", [128, TK], "bfloat16"),
-    "xe": ("sbuf", [128, TK], "bfloat16"),
+    "xe": ("sbuf", [128, WD], "bfloat16"),
     "nl": ("sbuf", [128, TK], "bfloat16"),
     "m": ("sbuf", [128, TK], "bfloat16"),
     "ys": ("sbuf", [128, TK], "bfloat16"),
@@ -22,7 +27,8 @@ SCRATCH = {
     "psq": ("psum", [128, 512], "float32"),
     "psy": ("psum", [128, 512], "float32"),
 }
-SEMAPHORES = ["le", "lx", "lw", "zs", "sa", "sn", "sh", "shr", "shn", "ae", "al", "sq", "sm", "snt", "sy", "yr", "st"]
+SEMAPHORES = ["le", "lx", "lw", "lt", "lp", "zs", "zq", "sa", "sn", "sh", "shr", "shn", "ae", "al", "sq", "sm", "snt",
+              "sy", "yr", "st"]
 
 
 def _same_chip(topo, a, b):
@@ -67,36 +73,44 @@ def rank_program(g, core, T, topo):
             if len(w) == 3 and w[1] == core:
                 n_in = _engines(topo, w[0], core)[1]
                 g.wait_ge(s.ae, n_in)
-                n = _send(g, T, topo, core, w[2], T.xe[:], T.xe[:], s.ae)
+                n = _send(g, T, topo, core, w[2], T.xe[:], T.xd[:], s.ae)
                 g.wait_ge(s.al, n_in)
                 n += _send(g, T, topo, core, w[2], T.nl[:], T.nl[:], s.al)
                 g.wait_ge(s.snt, n)
         return
 
-    def tile(buf, t):
-        return buf[:, t * TK:(t + 1) * TK]
+    def tile(buf, t, k=128):
+        return buf[0:k, t * TK:(t + 1) * TK]
 
     last = KT - 1
-    cut = last * TK
     nxt = ways[rank][1]
     n_in = _engines(topo, ways[(rank - 1) % n_ranks][-2], core)[1]
+    rest = 128 - CUT
+    two = ((g.sync, 0), (g.scalar, 1))
 
-    for q, lo, hi in ((g.sync, 0, 64), (g.scalar, 64, 128)):
-        q.dma_start(T.xs[lo:hi, cut:], T.x[lo:hi, cut:]).then_inc(s.le, 16)
-    for q, lo, hi in ((g.sync, 0, 64), (g.scalar, 64, 128)):
-        q.dma_start(T.xs[lo:hi, 0:cut], T.x[lo:hi, 0:cut]).then_inc(s.lx, 16)
-    for q, lo, hi in ((g.sync, 0, 64), (g.scalar, 64, 128)):
-        q.dma_start(T.ws[lo:hi, :], T.w[lo:hi, :]).then_inc(s.lw, 16)
     g.vector.memset(T.zero[:], 0.0).then_inc(s.zs, 1)
+    g.vector.memset(T.wq[:], 0.0).then_inc(s.zq, 1)
+    for q, i in two:
+        q.dma_start(T.xd[64 * i:64 * i + 64, :],
+                    T.x[CUT + i * rest // 2:CUT + (i + 1) * rest // 2, :]).then_inc(s.le, 16)
+    for q, i in two:
+        q.dma_start(T.xs[i * CUT // 2:(i + 1) * CUT // 2, :], T.x[i * CUT // 2:(i + 1) * CUT // 2, :]).then_inc(s.lx, 16)
+    for q, i in two:
+        q.dma_start(T.ws[i * CUT // 2:(i + 1) * CUT // 2, :], T.w[i * CUT // 2:(i + 1) * CUT // 2, :]).then_inc(s.lw, 16)
+    g.sync.dma_start(T.xs[CUT:128, :], T.x[CUT:128, :]).then_inc(s.lt, 16)
+    g.scalar.dma_start(T.ws[CUT:128, :], T.w[CUT:128, :]).then_inc(s.lt, 16)
+    for a in range(G):
+        q = two[a % 2][0]
+        q.wait_ge(s.zq, 1)
+        q.dma_start(T.wq[a:128:G, a * TK:(a + 1) * TK], T.w[CUT:128, :]).then_inc(s.lp, 16)
 
     g.wait_ge(s.le, 32)
-    n_out = _send(g, T, topo, core, nxt, T.xe[:], tile(T.xs, last), s.ae)
+    n_out = _send(g, T, topo, core, nxt, T.xe[:] if len(ways[rank]) == 2 else T.xd[:], T.xd[:], s.ae)
 
-    g.tensor.wait_ge(s.le, 32)
     g.tensor.wait_ge(s.lx, 32)
     g.tensor.wait_ge(s.lw, 32)
-    for t in range(last):
-        mm = g.tensor.matmul(T.psa[:, 0:TK], tile(T.ws, t), tile(T.xs, t), start=(t == 0), stop=(t == last - 1))
+    for t in range(KT):
+        mm = g.tensor.matmul(T.psa[:, 0:TK], tile(T.ws, t, CUT), tile(T.xs, t, CUT), start=(t == 0), stop=(t == last))
     mm.then_inc(s.sa, 1)
     g.vector.wait_ge(s.zs, 1)
     g.vector.wait_ge(s.sa, 1)
@@ -104,6 +118,7 @@ def rank_program(g, core, T, topo):
     g.wait_ge(s.sn, 1)
     n_out += _send(g, T, topo, core, nxt, T.nl[:], T.n1[:], s.al)
 
+    g.tensor.wait_ge(s.lt, 32)
     for t in range(KT):
         mm = g.tensor.matmul(T.psh[:, 0:TK], tile(T.ws, t), tile(T.xs, t), start=(t == 0), stop=(t == last))
     mm.then_inc(s.sh, 1)
@@ -112,14 +127,17 @@ def rank_program(g, core, T, topo):
     g.vector.wait_ge(s.shr, 1)
     g.vector.tensor_tensor(T.hn[:], T.zero[:], T.h[:], AluOpType.subtract).then_inc(s.shn, 1)
 
+    g.tensor.wait_ge(s.lp, 16 * G)
     g.tensor.wait_ge(s.ae, n_in)
-    g.tensor.matmul(T.psq[:, 0:TK], tile(T.ws, last), T.xe[:], start=True, stop=True).then_inc(s.sq, 1)
+    for a in range(G):
+        g.tensor.matmul(T.psq[:, a * WD:(a + 1) * WD], T.wq[:, a * TK:(a + 1) * TK], T.xe[:],
+                        start=True, stop=True).then_inc(s.sq, 1)
 
     g.tensor.wait_ge(s.shr, 1)
     g.tensor.wait_ge(s.shn, 1)
     g.tensor.wait_ge(s.al, n_in)
     g.tensor.matmul(T.psy[:, 0:TK], T.nl[:], T.hn[:], start=True, stop=False)
-    g.vector.wait_ge(s.sq, 1)
+    g.vector.wait_ge(s.sq, G)
     g.vector.wait_ge(s.al, n_in)
     g.vector.tensor_tensor(T.m[:], T.psq[:, 0:TK], T.nl[:], AluOpType.max).then_inc(s.sm, 1)
     g.tensor.wait_ge(s.sm, 1)

@@ -6,6 +6,8 @@ KT = 4
 CUT = 112
 WD = (128 - CUT) * KT * TK // 128
 G = TK // WD
+PAD = TK - WD
+HF = TK // 2
 ENG_CHIP = 8
 ENG_OUT = 8
 
@@ -14,21 +16,27 @@ SCRATCH = {
     "ws": ("sbuf", [128, KT * TK], "bfloat16"),
     "wq": ("sbuf", [128, G * TK], "bfloat16"),
     "xd": ("dram", [128, WD], "bfloat16"),
-    "zero": ("sbuf", [128, TK], "float32"),
+    "xo": ("sbuf", [128, WD], "bfloat16"),
+    "qo": ("sbuf", [128, TK], "float32"),
     "n1": ("sbuf", [128, TK], "bfloat16"),
     "h": ("sbuf", [128, TK], "bfloat16"),
-    "hn": ("sbuf", [128, TK], "bfloat16"),
-    "xe": ("sbuf", [128, WD], "bfloat16"),
+    "ones": ("sbuf", [128, TK], "bfloat16"),
+    "ident": ("sbuf", [128, TK], "bfloat16"),
+    "wt": ("sbuf", [128, G * TK], "bfloat16"),
+    "v": ("sbuf", [128, G * TK], "bfloat16"),
+    "z": ("sbuf", [128, PAD + WD + PAD], "bfloat16"),
     "nl": ("sbuf", [128, TK], "bfloat16"),
-    "m": ("sbuf", [128, TK], "bfloat16"),
     "ys": ("sbuf", [128, TK], "bfloat16"),
     "psa": ("psum", [128, 512], "float32"),
     "psh": ("psum", [128, 512], "float32"),
-    "psq": ("psum", [128, 512], "float32"),
-    "psy": ("psum", [128, 512], "float32"),
+    "psqo": ("psum", [128, 512], "float32"),
+    "pst": ("psum", [128, 512], "float32"),
+    "psv": ("psum", [128, 512], "float32"),
+    "psy0": ("psum", [128, 512], "float32"),
+    "psy1": ("psum", [128, 512], "float32"),
 }
-SEMAPHORES = ["le", "lx", "lw", "lt", "lp", "zs", "zq", "sa", "sn", "sh", "shr", "shn", "ae", "al", "sq", "sm", "snt",
-              "sy", "yr", "st"]
+SEMAPHORES = ["le", "lq", "lx", "lt", "zq", "zo", "zz", "si", "so", "sqo", "sa", "sh", "sn", "shr", "tt", "tc", "sv", "vc",
+              "ae", "al", "sy0", "sy1", "yr0", "yr1", "st0", "st1", "snt"]
 
 
 def _same_chip(topo, a, b):
@@ -67,13 +75,14 @@ def rank_program(g, core, T, topo):
     ways = [_way(topo, T, cores[r], cores[(r + 1) % n_ranks]) for r in range(n_ranks)]
     rank = T.rank_of(core)
     s = T.sem
+    land = T.z[:, PAD:PAD + WD]
 
     if rank is None:
         for w in ways:
             if len(w) == 3 and w[1] == core:
                 n_in = _engines(topo, w[0], core)[1]
                 g.wait_ge(s.ae, n_in)
-                n = _send(g, T, topo, core, w[2], T.xe[:], T.xd[:], s.ae)
+                n = _send(g, T, topo, core, w[2], land, T.xd[:], s.ae)
                 g.wait_ge(s.al, n_in)
                 n += _send(g, T, topo, core, w[2], T.nl[:], T.nl[:], s.al)
                 g.wait_ge(s.snt, n)
@@ -88,33 +97,46 @@ def rank_program(g, core, T, topo):
     rest = 128 - CUT
     two = ((g.sync, 0), (g.scalar, 1))
 
-    g.vector.memset(T.zero[:], 0.0).then_inc(s.zs, 1)
     g.vector.memset(T.wq[:], 0.0).then_inc(s.zq, 1)
+    g.vector.memset(T.ones[:], 1.0).then_inc(s.zo, 1)
+    g.vector.memset(T.z[:, 0:PAD], 0.0).then_inc(s.zz, 1)
+    g.vector.memset(T.z[:, PAD + WD:PAD + WD + PAD], 0.0).then_inc(s.zz, 1)
     for q, i in two:
         q.dma_start(T.xd[64 * i:64 * i + 64, :],
                     T.x[CUT + i * rest // 2:CUT + (i + 1) * rest // 2, :]).then_inc(s.le, 16)
     for q, i in two:
-        q.dma_start(T.xs[i * CUT // 2:(i + 1) * CUT // 2, :], T.x[i * CUT // 2:(i + 1) * CUT // 2, :]).then_inc(s.lx, 16)
-    for q, i in two:
-        q.dma_start(T.ws[i * CUT // 2:(i + 1) * CUT // 2, :], T.w[i * CUT // 2:(i + 1) * CUT // 2, :]).then_inc(s.lw, 16)
-    g.sync.dma_start(T.xs[CUT:128, :], T.x[CUT:128, :]).then_inc(s.lt, 16)
-    g.scalar.dma_start(T.ws[CUT:128, :], T.w[CUT:128, :]).then_inc(s.lt, 16)
+        q.dma_start(T.xo[64 * i:64 * i + 64, :],
+                    T.x[CUT + i * rest // 2:CUT + (i + 1) * rest // 2, :]).then_inc(s.lq, 16)
     for a in range(G):
         q = two[a % 2][0]
         q.wait_ge(s.zq, 1)
-        q.dma_start(T.wq[a:128:G, a * TK:(a + 1) * TK], T.w[CUT:128, :]).then_inc(s.lp, 16)
+        q.dma_start(T.wq[a:128:G, a * TK:(a + 1) * TK], T.w[CUT:128, :]).then_inc(s.lq, 16)
+    for q, i in two:
+        q.dma_start(T.xs[i * CUT // 2:(i + 1) * CUT // 2, :], T.x[i * CUT // 2:(i + 1) * CUT // 2, :]).then_inc(s.lx, 16)
+    for q, i in two:
+        q.dma_start(T.ws[i * CUT // 2:(i + 1) * CUT // 2, :], T.w[i * CUT // 2:(i + 1) * CUT // 2, :]).then_inc(s.lx, 16)
+    g.sync.dma_start(T.xs[CUT:128, :], T.x[CUT:128, :]).then_inc(s.lt, 16)
+    g.scalar.dma_start(T.ws[CUT:128, :], T.w[CUT:128, :]).then_inc(s.lt, 16)
 
     g.wait_ge(s.le, 32)
-    n_out = _send(g, T, topo, core, nxt, T.xe[:] if len(ways[rank]) == 2 else T.xd[:], T.xd[:], s.ae)
+    n_out = _send(g, T, topo, core, nxt, land if len(ways[rank]) == 2 else T.xd[:], T.xd[:], s.ae)
+    g.wait_ge(s.zo, 1)
+    g.affine_select(T.ident[:], T.ones[:], [[-1, TK]], AluOpType.is_equal, 0.0, 0, 1).then_inc(s.si, 1)
 
-    g.tensor.wait_ge(s.lx, 32)
-    g.tensor.wait_ge(s.lw, 32)
+    g.tensor.wait_ge(s.lq, 32 + 16 * G)
+    for a in range(G):
+        g.tensor.matmul(T.psqo[:, a * WD:(a + 1) * WD], T.wq[:, a * TK:(a + 1) * TK], T.xo[:],
+                        start=True, stop=True).then_inc(s.so, 1)
+    g.vector.wait_ge(s.so, G)
+    g.vector.tensor_scalar(T.qo[:], T.psqo[:, 0:TK], -1.0, None, AluOpType.mult).then_inc(s.sqo, 1)
+
+    g.tensor.wait_ge(s.lx, 64)
     for t in range(KT):
         mm = g.tensor.matmul(T.psa[:, 0:TK], tile(T.ws, t, CUT), tile(T.xs, t, CUT), start=(t == 0), stop=(t == last))
     mm.then_inc(s.sa, 1)
-    g.vector.wait_ge(s.zs, 1)
+    g.vector.wait_ge(s.sqo, 1)
     g.vector.wait_ge(s.sa, 1)
-    g.vector.tensor_tensor(T.n1[:], T.zero[:], T.psa[:, 0:TK], AluOpType.subtract).then_inc(s.sn, 1)
+    g.vector.tensor_tensor(T.n1[:], T.psa[:, 0:TK], T.qo[:], AluOpType.max).then_inc(s.sn, 1)
     g.wait_ge(s.sn, 1)
     n_out += _send(g, T, topo, core, nxt, T.nl[:], T.n1[:], s.al)
 
@@ -123,28 +145,37 @@ def rank_program(g, core, T, topo):
         mm = g.tensor.matmul(T.psh[:, 0:TK], tile(T.ws, t), tile(T.xs, t), start=(t == 0), stop=(t == last))
     mm.then_inc(s.sh, 1)
     g.vector.wait_ge(s.sh, 1)
-    g.vector.tensor_tensor(T.h[:], T.psh[:, 0:TK], T.zero[:], AluOpType.max).then_inc(s.shr, 1)
-    g.vector.wait_ge(s.shr, 1)
-    g.vector.tensor_tensor(T.hn[:], T.zero[:], T.h[:], AluOpType.subtract).then_inc(s.shn, 1)
+    g.vector.tensor_scalar(T.h[:], T.psh[:, 0:TK], 0.0, None, AluOpType.max).then_inc(s.shr, 1)
 
-    g.tensor.wait_ge(s.lp, 16 * G)
-    g.tensor.wait_ge(s.ae, n_in)
+    g.tensor.wait_ge(s.si, 1)
     for a in range(G):
-        g.tensor.matmul(T.psq[:, a * WD:(a + 1) * WD], T.wq[:, a * TK:(a + 1) * TK], T.xe[:],
-                        start=True, stop=True).then_inc(s.sq, 1)
-
+        g.tensor.matmul(T.pst[:, a * TK:(a + 1) * TK], T.wq[:, a * TK:(a + 1) * TK], T.ident[:],
+                        start=True, stop=True).then_inc(s.tt, 1)
+    g.vector.wait_ge(s.tt, G)
+    g.vector.tensor_copy(T.wt[:], T.pst[:, 0:G * TK]).then_inc(s.tc, 1)
+    g.tensor.wait_ge(s.tc, 1)
     g.tensor.wait_ge(s.shr, 1)
-    g.tensor.wait_ge(s.shn, 1)
+    for a in range(G):
+        g.tensor.matmul(T.psv[:, a * TK:(a + 1) * TK], T.wt[:, a * TK:(a + 1) * TK], T.h[:],
+                        start=True, stop=True).then_inc(s.sv, 1)
+    g.vector.wait_ge(s.sv, G)
+    g.vector.tensor_copy(T.v[:], T.psv[:, 0:G * TK]).then_inc(s.vc, 1)
+
+    psy, sy, yr, st = (T.psy0, T.psy1), (s.sy0, s.sy1), (s.yr0, s.yr1), (s.st0, s.st1)
+    g.tensor.wait_ge(s.zz, 2)
+    g.tensor.wait_ge(s.vc, 1)
+    g.tensor.wait_ge(s.ae, n_in)
+    for i in range(2):
+        for a in range(G):
+            g.tensor.matmul(psy[i][:, 0:HF], T.z[:, PAD - a * WD:PAD - a * WD + TK],
+                            T.v[:, a * TK + i * HF:a * TK + (i + 1) * HF], start=(a == 0), stop=False)
     g.tensor.wait_ge(s.al, n_in)
-    g.tensor.matmul(T.psy[:, 0:TK], T.nl[:], T.hn[:], start=True, stop=False)
-    g.vector.wait_ge(s.sq, G)
-    g.vector.wait_ge(s.al, n_in)
-    g.vector.tensor_tensor(T.m[:], T.psq[:, 0:TK], T.nl[:], AluOpType.max).then_inc(s.sm, 1)
-    g.tensor.wait_ge(s.sm, 1)
-    g.tensor.matmul(T.psy[:, 0:TK], T.m[:], T.h[:], start=False, stop=True).then_inc(s.sy, 1)
-    g.vector.wait_ge(s.sy, 1)
-    g.vector.tensor_copy(T.ys[:], T.psy[:, 0:TK]).then_inc(s.yr, 1)
-    g.sync.wait_ge(s.yr, 1)
-    g.sync.dma_start(T.y[:], T.ys[:]).then_inc(s.st, 16)
-    g.sync.wait_ge(s.st, 16)
+    for i in range(2):
+        g.tensor.matmul(psy[i][:, 0:HF], T.nl[:], T.h[:, i * HF:(i + 1) * HF], start=False, stop=True).then_inc(sy[i], 1)
+    for q, i in two:
+        g.vector.wait_ge(sy[i], 1)
+        g.vector.tensor_copy(T.ys[:, i * HF:(i + 1) * HF], psy[i][:, 0:HF]).then_inc(yr[i], 1)
+        q.wait_ge(yr[i], 1)
+        q.dma_start(T.y[:, i * HF:(i + 1) * HF], T.ys[:, i * HF:(i + 1) * HF]).then_inc(st[i], 16)
+        q.wait_ge(st[i], 16)
     g.wait_ge(s.snt, n_out)

@@ -1,4 +1,4 @@
-from concourse.mybir import AluOpType
+from concourse.mybir import AluOpType, ActivationFunctionType
 
 SIM_CORES = 256
 TK = 128
@@ -8,6 +8,7 @@ WD = (128 - CUT) * KT * TK // 128
 G = TK // WD
 PAD = TK - WD
 HF = TK // 2
+SPL = 64
 ENG_CHIP = 8
 ENG_OUT = 8
 
@@ -16,7 +17,8 @@ SCRATCH = {
     "ws": ("sbuf", [128, KT * TK], "bfloat16"),
     "wq": ("sbuf", [128, G * TK], "bfloat16"),
     "xd": ("dram", [128, WD], "bfloat16"),
-    "xo": ("sbuf", [128, WD], "bfloat16"),
+    "xt": ("sbuf", [128, KT * TK], "bfloat16"),
+    "wl": ("sbuf", [128, KT * TK], "bfloat16"),
     "qo": ("sbuf", [128, TK], "float32"),
     "n1": ("sbuf", [128, TK], "bfloat16"),
     "h": ("sbuf", [128, TK], "bfloat16"),
@@ -35,8 +37,8 @@ SCRATCH = {
     "psy0": ("psum", [128, 512], "float32"),
     "psy1": ("psum", [128, 512], "float32"),
 }
-SEMAPHORES = ["le", "lq", "lx", "lt", "zq", "zo", "zz", "si", "so", "sqo", "sa", "sh", "sn", "shr", "tt", "tc", "sv", "vc",
-              "ae", "al", "sy0", "sy1", "yr0", "yr1", "st0", "st1", "snt"]
+SEMAPHORES = ["le", "lq", "lx", "lw", "zq", "zo", "zz", "si", "so", "sqo", "sa", "sh", "sn", "shr", "tt", "tc", "sv", "vc",
+              "ae", "al", "sy0", "sy1", "yr", "st", "snt"]
 
 
 def _same_chip(topo, a, b):
@@ -69,6 +71,13 @@ def _send(g, T, topo, core, dst, out_ap, src_ap, sem):
     return n
 
 
+def _identity(g, T):
+    s = T.sem
+    g.vector.memset(T.ones[:], 1.0).then_inc(s.zo, 1)
+    g.wait_ge(s.zo, 1)
+    g.affine_select(T.ident[:], T.ones[:], [[-1, TK]], AluOpType.is_equal, 0.0, 0, 1).then_inc(s.si, 1)
+
+
 def rank_program(g, core, T, topo):
     cores = list(T.cores)
     n_ranks = len(cores)
@@ -81,14 +90,19 @@ def rank_program(g, core, T, topo):
         for w in ways:
             if len(w) == 3 and w[1] == core:
                 n_in = _engines(topo, w[0], core)[1]
+                m, n = _engines(topo, core, w[2])
+                _identity(g, T)
+                g.wait_ge(s.si, 1)
+                rid, pid = topo.addr(w[0], core)
+                g.remote_dma(T.ident[:], T.ident[:], s.si, s.snt, pid, rid, m & topo.mask(core, w[0]))
                 g.wait_ge(s.ae, n_in)
-                n = _send(g, T, topo, core, w[2], land, T.xd[:], s.ae)
+                n += _send(g, T, topo, core, w[2], land, T.xd[:], s.ae)
                 g.wait_ge(s.al, n_in)
                 n += _send(g, T, topo, core, w[2], T.nl[:], T.nl[:], s.al)
                 g.wait_ge(s.snt, n)
         return
 
-    def tile(buf, t, k=128):
+    def tile(buf, t, k):
         return buf[0:k, t * TK:(t + 1) * TK]
 
     last = KT - 1
@@ -96,38 +110,38 @@ def rank_program(g, core, T, topo):
     n_in = _engines(topo, ways[(rank - 1) % n_ranks][-2], core)[1]
     rest = 128 - CUT
     two = ((g.sync, 0), (g.scalar, 1))
+    passed = len(ways[rank]) == 3
+    n_si = _engines(topo, ways[rank][1], ways[rank][2])[1] if passed else 1
 
     g.vector.memset(T.wq[:], 0.0).then_inc(s.zq, 1)
-    g.vector.memset(T.ones[:], 1.0).then_inc(s.zo, 1)
     g.vector.memset(T.z[:, 0:PAD], 0.0).then_inc(s.zz, 1)
     g.vector.memset(T.z[:, PAD + WD:PAD + WD + PAD], 0.0).then_inc(s.zz, 1)
     for q, i in two:
         q.dma_start(T.xd[64 * i:64 * i + 64, :],
                     T.x[CUT + i * rest // 2:CUT + (i + 1) * rest // 2, :]).then_inc(s.le, 16)
-    for q, i in two:
-        q.dma_start(T.xo[64 * i:64 * i + 64, :],
-                    T.x[CUT + i * rest // 2:CUT + (i + 1) * rest // 2, :]).then_inc(s.lq, 16)
+    g.sync.dma_start(T.xt[0:rest, :], T.x[CUT:128, :]).then_inc(s.lq, 16)
+    g.scalar.dma_start(T.wl[0:rest, :], T.w[CUT:128, :]).then_inc(s.lq, 16)
+    g.sync.dma_start(T.xs[0:SPL, :], T.x[0:SPL, :]).then_inc(s.lx, 16)
+    g.scalar.dma_start(T.xs[SPL:CUT, :], T.x[SPL:CUT, :]).then_inc(s.lx, 16)
+    g.scalar.dma_start(T.ws[0:SPL, :], T.w[0:SPL, :]).then_inc(s.lx, 16)
+    g.sync.dma_start(T.ws[SPL:CUT, :], T.w[SPL:CUT, :]).then_inc(s.lx, 16)
     for a in range(G):
         q = two[a % 2][0]
         q.wait_ge(s.zq, 1)
-        q.dma_start(T.wq[a:128:G, a * TK:(a + 1) * TK], T.w[CUT:128, :]).then_inc(s.lq, 16)
-    for q, i in two:
-        q.dma_start(T.xs[i * CUT // 2:(i + 1) * CUT // 2, :], T.x[i * CUT // 2:(i + 1) * CUT // 2, :]).then_inc(s.lx, 16)
-    for q, i in two:
-        q.dma_start(T.ws[i * CUT // 2:(i + 1) * CUT // 2, :], T.w[i * CUT // 2:(i + 1) * CUT // 2, :]).then_inc(s.lx, 16)
-    g.sync.dma_start(T.xs[CUT:128, :], T.x[CUT:128, :]).then_inc(s.lt, 16)
-    g.scalar.dma_start(T.ws[CUT:128, :], T.w[CUT:128, :]).then_inc(s.lt, 16)
+        q.dma_start(T.wq[a:128:G, a * TK:(a + 1) * TK], T.w[CUT:128, :]).then_inc(s.lw, 16)
 
     g.wait_ge(s.le, 32)
-    n_out = _send(g, T, topo, core, nxt, land if len(ways[rank]) == 2 else T.xd[:], T.xd[:], s.ae)
-    g.wait_ge(s.zo, 1)
-    g.affine_select(T.ident[:], T.ones[:], [[-1, TK]], AluOpType.is_equal, 0.0, 0, 1).then_inc(s.si, 1)
+    n_out = _send(g, T, topo, core, nxt, T.xd[:] if passed else land, T.xd[:], s.ae)
+    if not passed:
+        _identity(g, T)
 
-    g.tensor.wait_ge(s.lq, 32 + 16 * G)
-    for a in range(G):
-        g.tensor.matmul(T.psqo[:, a * WD:(a + 1) * WD], T.wq[:, a * TK:(a + 1) * TK], T.xo[:],
-                        start=True, stop=True).then_inc(s.so, 1)
-    g.vector.wait_ge(s.so, G)
+    g.tensor.wait_ge(s.lq, 32)
+    for t in range(KT):
+        mm = g.tensor.matmul(T.psqo[:, 0:TK], tile(T.wl, t, rest), tile(T.xt, t, rest), start=(t == 0), stop=(t == last))
+    mm.then_inc(s.so, 1)
+    for t in range(KT):
+        g.tensor.matmul(T.psh[:, 0:TK], tile(T.wl, t, rest), tile(T.xt, t, rest), start=(t == 0), stop=False)
+    g.vector.wait_ge(s.so, 1)
     g.vector.tensor_scalar(T.qo[:], T.psqo[:, 0:TK], -1.0, None, AluOpType.mult).then_inc(s.sqo, 1)
 
     g.tensor.wait_ge(s.lx, 64)
@@ -140,14 +154,14 @@ def rank_program(g, core, T, topo):
     g.wait_ge(s.sn, 1)
     n_out += _send(g, T, topo, core, nxt, T.nl[:], T.n1[:], s.al)
 
-    g.tensor.wait_ge(s.lt, 32)
     for t in range(KT):
-        mm = g.tensor.matmul(T.psh[:, 0:TK], tile(T.ws, t), tile(T.xs, t), start=(t == 0), stop=(t == last))
+        mm = g.tensor.matmul(T.psh[:, 0:TK], tile(T.ws, t, CUT), tile(T.xs, t, CUT), start=False, stop=(t == last))
     mm.then_inc(s.sh, 1)
     g.vector.wait_ge(s.sh, 1)
     g.vector.tensor_scalar(T.h[:], T.psh[:, 0:TK], 0.0, None, AluOpType.max).then_inc(s.shr, 1)
 
-    g.tensor.wait_ge(s.si, 1)
+    g.tensor.wait_ge(s.si, n_si)
+    g.tensor.wait_ge(s.lw, 16 * G)
     for a in range(G):
         g.tensor.matmul(T.pst[:, a * TK:(a + 1) * TK], T.wq[:, a * TK:(a + 1) * TK], T.ident[:],
                         start=True, stop=True).then_inc(s.tt, 1)
@@ -161,7 +175,7 @@ def rank_program(g, core, T, topo):
     g.vector.wait_ge(s.sv, G)
     g.vector.tensor_copy(T.v[:], T.psv[:, 0:G * TK]).then_inc(s.vc, 1)
 
-    psy, sy, yr, st = (T.psy0, T.psy1), (s.sy0, s.sy1), (s.yr0, s.yr1), (s.st0, s.st1)
+    psy, sy = (T.psy0, T.psy1), (s.sy0, s.sy1)
     g.tensor.wait_ge(s.zz, 2)
     g.tensor.wait_ge(s.vc, 1)
     g.tensor.wait_ge(s.ae, n_in)
@@ -172,10 +186,11 @@ def rank_program(g, core, T, topo):
     g.tensor.wait_ge(s.al, n_in)
     for i in range(2):
         g.tensor.matmul(psy[i][:, 0:HF], T.nl[:], T.h[:, i * HF:(i + 1) * HF], start=False, stop=True).then_inc(sy[i], 1)
-    for q, i in two:
-        g.vector.wait_ge(sy[i], 1)
-        g.vector.tensor_copy(T.ys[:, i * HF:(i + 1) * HF], psy[i][:, 0:HF]).then_inc(yr[i], 1)
-        q.wait_ge(yr[i], 1)
-        q.dma_start(T.y[:, i * HF:(i + 1) * HF], T.ys[:, i * HF:(i + 1) * HF]).then_inc(st[i], 16)
-        q.wait_ge(st[i], 16)
+    g.vector.wait_ge(sy[0], 1)
+    g.vector.tensor_copy(T.ys[:, 0:HF], psy[0][:, 0:HF]).then_inc(s.yr, 1)
+    g.scalar.wait_ge(sy[1], 1)
+    g.scalar.activation(T.ys[:, HF:TK], psy[1][:, 0:HF], ActivationFunctionType.Copy).then_inc(s.yr, 1)
+    g.sync.wait_ge(s.yr, 2)
+    g.sync.dma_start(T.y[:], T.ys[:]).then_inc(s.st, 16)
+    g.sync.wait_ge(s.st, 16)
     g.wait_ge(s.snt, n_out)

@@ -6,9 +6,8 @@ KT = 4
 CUT = 112
 WD = (128 - CUT) * KT * TK // 128
 G = TK // WD
-PAD = TK - WD
 HF = TK // 2
-SPL = 64
+EB = G - 1
 ENG_CHIP = 8
 ENG_OUT = 8
 
@@ -21,24 +20,28 @@ SCRATCH = {
     "wl": ("sbuf", [128, KT * TK], "bfloat16"),
     "qo": ("sbuf", [128, TK], "float32"),
     "n1": ("sbuf", [128, TK], "bfloat16"),
+    "hm": ("sbuf", [128, TK], "float32"),
     "h": ("sbuf", [128, TK], "bfloat16"),
     "ones": ("sbuf", [128, TK], "bfloat16"),
     "ident": ("sbuf", [128, TK], "bfloat16"),
     "wt": ("sbuf", [128, G * TK], "bfloat16"),
     "v": ("sbuf", [128, G * TK], "bfloat16"),
-    "z": ("sbuf", [128, PAD + WD + PAD], "bfloat16"),
+    "blk": ("sbuf", [128, WD], "bfloat16"),
     "nl": ("sbuf", [128, TK], "bfloat16"),
-    "ys": ("sbuf", [128, TK], "bfloat16"),
-    "psa": ("psum", [128, 512], "float32"),
-    "psh": ("psum", [128, 512], "float32"),
+    "ys0": ("sbuf", [128, TK], "bfloat16"),
+    "ys1": ("sbuf", [128, TK], "bfloat16"),
     "psqo": ("psum", [128, 512], "float32"),
-    "pst": ("psum", [128, 512], "float32"),
-    "psv": ("psum", [128, 512], "float32"),
+    "psa0": ("psum", [128, 512], "float32"),
+    "psa1": ("psum", [128, 512], "float32"),
+    "pv0": ("psum", [128, 512], "float32"),
+    "pv1": ("psum", [128, 512], "float32"),
     "psy0": ("psum", [128, 512], "float32"),
     "psy1": ("psum", [128, 512], "float32"),
+    "psy2": ("psum", [128, 512], "float32"),
 }
-SEMAPHORES = ["le", "lq", "lx", "lw", "zq", "zo", "zz", "si", "so", "sqo", "sa", "sh", "sn", "shr", "tt", "tc", "sv", "vc",
-              "ae", "al", "sy0", "sy1", "yr", "st", "snt"]
+SEMAPHORES = ["le", "lq", "lx", "lw", "zq", "zo", "si", "so", "sqo", "sa0", "sa1", "sn0", "sn1", "sm0", "sm1", "shr",
+              "tt0", "tt1", "tc0", "tc1", "sv0", "sv1", "vc0", "vc1", "ae", "al0", "al1",
+              "sy00", "sy01", "sy10", "sy11", "yr0", "yr1", "st0", "st1", "snt"]
 
 
 def _same_chip(topo, a, b):
@@ -57,11 +60,11 @@ def _engines(topo, src, dst):
 
 def _way(topo, T, src, dst):
     if topo.may_write(src, dst):
-        return [src, dst]
+        return src, [], dst
     c = [k for k in range(SIM_CORES)
          if k != src and T.rank_of(k) is None and _same_chip(topo, k, src) and topo.may_write(k, dst)]
     c.sort(key=lambda k: (topo.die(k) != topo.die(src), k))
-    return [src, c[0], dst]
+    return src, c[:G], dst
 
 
 def _send(g, T, topo, core, dst, out_ap, src_ap, sem):
@@ -71,11 +74,11 @@ def _send(g, T, topo, core, dst, out_ap, src_ap, sem):
     return n
 
 
-def _identity(g, T):
+def _identity(g, T, c0, c1):
     s = T.sem
-    g.vector.memset(T.ones[:], 1.0).then_inc(s.zo, 1)
+    g.vector.memset(T.ones[:, c0:c1], 1.0).then_inc(s.zo, 1)
     g.wait_ge(s.zo, 1)
-    g.affine_select(T.ident[:], T.ones[:], [[-1, TK]], AluOpType.is_equal, 0.0, 0, 1).then_inc(s.si, 1)
+    g.affine_select(T.ident[:, c0:c1], T.ones[:, c0:c1], [[-1, c1 - c0]], AluOpType.is_equal, 0.0, -c0, 1).then_inc(s.si, 1)
 
 
 def rank_program(g, core, T, topo):
@@ -84,21 +87,26 @@ def rank_program(g, core, T, topo):
     ways = [_way(topo, T, cores[r], cores[(r + 1) % n_ranks]) for r in range(n_ranks)]
     rank = T.rank_of(core)
     s = T.sem
-    land = T.z[:, PAD:PAD + WD]
+    al = (s.al0, s.al1)
+
+    def half(buf, a):
+        return buf[:, a * HF:(a + 1) * HF]
 
     if rank is None:
-        for w in ways:
-            if len(w) == 3 and w[1] == core:
-                n_in = _engines(topo, w[0], core)[1]
-                m, n = _engines(topo, core, w[2])
-                _identity(g, T)
+        for src, mid, dst in ways:
+            if core in mid:
+                a = mid.index(core)
+                n_in = _engines(topo, src, core)[1]
+                m, n = _engines(topo, core, dst)
+                _identity(g, T, a * HF, (a + 1) * HF)
                 g.wait_ge(s.si, 1)
-                rid, pid = topo.addr(w[0], core)
-                g.remote_dma(T.ident[:], T.ident[:], s.si, s.snt, pid, rid, m & topo.mask(core, w[0]))
-                g.wait_ge(s.ae, n_in)
-                n += _send(g, T, topo, core, w[2], land, T.xd[:], s.ae)
-                g.wait_ge(s.al, n_in)
-                n += _send(g, T, topo, core, w[2], T.nl[:], T.nl[:], s.al)
+                rid, pid = topo.addr(src, core)
+                g.remote_dma(half(T.ident, a), half(T.ident, a), s.si, s.snt, pid, rid, m & topo.mask(core, src))
+                if a == EB:
+                    g.wait_ge(s.ae, n_in)
+                    n += _send(g, T, topo, core, dst, T.blk[:], T.xd[:], s.ae)
+                g.wait_ge(al[a], n_in)
+                n += _send(g, T, topo, core, dst, half(T.nl, a), half(T.nl, a), al[a])
                 g.wait_ge(s.snt, n)
         return
 
@@ -106,91 +114,96 @@ def rank_program(g, core, T, topo):
         return buf[0:k, t * TK:(t + 1) * TK]
 
     last = KT - 1
-    nxt = ways[rank][1]
-    n_in = _engines(topo, ways[(rank - 1) % n_ranks][-2], core)[1]
+    _, mid, nxt = ways[rank]
+    psrc, pmid, _ = ways[(rank - 1) % n_ranks]
+    n_in = _engines(topo, pmid[0] if pmid else psrc, core)[1]
+    al_in = al if pmid else (s.al1, s.al1)
     rest = 128 - CUT
-    two = ((g.sync, 0), (g.scalar, 1))
-    passed = len(ways[rank]) == 3
-    n_si = _engines(topo, ways[rank][1], ways[rank][2])[1] if passed else 1
+    n_si = sum(_engines(topo, k, nxt)[1] for k in mid) if mid else 1
 
     g.vector.memset(T.wq[:], 0.0).then_inc(s.zq, 1)
-    g.vector.memset(T.z[:, 0:PAD], 0.0).then_inc(s.zz, 1)
-    g.vector.memset(T.z[:, PAD + WD:PAD + WD + PAD], 0.0).then_inc(s.zz, 1)
-    for q, i in two:
-        q.dma_start(T.xd[64 * i:64 * i + 64, :],
-                    T.x[CUT + i * rest // 2:CUT + (i + 1) * rest // 2, :]).then_inc(s.le, 16)
-    g.sync.dma_start(T.xt[0:rest, :], T.x[CUT:128, :]).then_inc(s.lq, 16)
+    g.sync.dma_start(T.xd[:], T.x[CUT:128, :]).then_inc(s.le, 16)
     g.scalar.dma_start(T.wl[0:rest, :], T.w[CUT:128, :]).then_inc(s.lq, 16)
-    g.sync.dma_start(T.xs[0:SPL, :], T.x[0:SPL, :]).then_inc(s.lx, 16)
-    g.scalar.dma_start(T.xs[SPL:CUT, :], T.x[SPL:CUT, :]).then_inc(s.lx, 16)
-    g.scalar.dma_start(T.ws[0:SPL, :], T.w[0:SPL, :]).then_inc(s.lx, 16)
-    g.sync.dma_start(T.ws[SPL:CUT, :], T.w[SPL:CUT, :]).then_inc(s.lx, 16)
-    for a in range(G):
-        q = two[a % 2][0]
+    g.sync.dma_start(T.xt[0:rest, :], T.x[CUT:128, :]).then_inc(s.lq, 16)
+    g.scalar.dma_start(T.ws[0:CUT, :], T.w[0:CUT, :]).then_inc(s.lx, 16)
+    g.sync.dma_start(T.xs[0:CUT, :], T.x[0:CUT, :]).then_inc(s.lx, 16)
+    for a, q in enumerate((g.sync, g.scalar)):
         q.wait_ge(s.zq, 1)
         q.dma_start(T.wq[a:128:G, a * TK:(a + 1) * TK], T.w[CUT:128, :]).then_inc(s.lw, 16)
 
-    g.wait_ge(s.le, 32)
-    n_out = _send(g, T, topo, core, nxt, T.xd[:] if passed else land, T.xd[:], s.ae)
-    if not passed:
-        _identity(g, T)
+    if not mid:
+        _identity(g, T, 0, TK)
+    g.wait_ge(s.le, 16)
+    if mid:
+        n_out = _send(g, T, topo, core, mid[EB], T.xd[:], T.xd[:], s.ae)
+    else:
+        n_out = _send(g, T, topo, core, nxt, T.blk[:], T.xd[:], s.ae)
 
     g.tensor.wait_ge(s.lq, 32)
     for t in range(KT):
         mm = g.tensor.matmul(T.psqo[:, 0:TK], tile(T.wl, t, rest), tile(T.xt, t, rest), start=(t == 0), stop=(t == last))
     mm.then_inc(s.so, 1)
-    for t in range(KT):
-        g.tensor.matmul(T.psh[:, 0:TK], tile(T.wl, t, rest), tile(T.xt, t, rest), start=(t == 0), stop=False)
     g.vector.wait_ge(s.so, 1)
     g.vector.tensor_scalar(T.qo[:], T.psqo[:, 0:TK], -1.0, None, AluOpType.mult).then_inc(s.sqo, 1)
 
-    g.tensor.wait_ge(s.lx, 64)
-    for t in range(KT):
-        mm = g.tensor.matmul(T.psa[:, 0:TK], tile(T.ws, t, CUT), tile(T.xs, t, CUT), start=(t == 0), stop=(t == last))
-    mm.then_inc(s.sa, 1)
+    psa, sa, sn, sm = (T.psa0, T.psa1), (s.sa0, s.sa1), (s.sn0, s.sn1), (s.sm0, s.sm1)
+    g.tensor.wait_ge(s.lx, 32)
     g.vector.wait_ge(s.sqo, 1)
-    g.vector.wait_ge(s.sa, 1)
-    g.vector.tensor_tensor(T.n1[:], T.psa[:, 0:TK], T.qo[:], AluOpType.max).then_inc(s.sn, 1)
-    g.wait_ge(s.sn, 1)
-    n_out += _send(g, T, topo, core, nxt, T.nl[:], T.n1[:], s.al)
+    for a in range(G):
+        for t in range(KT):
+            mm = g.tensor.matmul(psa[a][:, 0:HF], tile(T.ws, t, CUT), T.xs[0:CUT, t * TK + a * HF:t * TK + (a + 1) * HF],
+                                 start=(t == 0), stop=(t == last))
+        mm.then_inc(sa[a], 1)
+        g.vector.wait_ge(sa[a], 1)
+        g.vector.tensor_tensor(half(T.n1, a), psa[a][:, 0:HF], half(T.qo, a), AluOpType.max).then_inc(sn[a], 1)
+        g.vector.tensor_tensor(half(T.hm, a), psa[a][:, 0:HF], half(T.qo, a), AluOpType.subtract).then_inc(sm[a], 1)
+        g.scalar.wait_ge(sm[a], 1)
+        g.scalar.activation(half(T.h, a), half(T.hm, a), ActivationFunctionType.Relu).then_inc(s.shr, 1)
+        g.wait_ge(sn[a], 1)
+        if mid:
+            n_out += _send(g, T, topo, core, mid[a], half(T.nl, a), half(T.n1, a), al[a])
+    if not mid:
+        n_out += _send(g, T, topo, core, nxt, T.nl[:], T.n1[:], s.al1)
 
-    for t in range(KT):
-        mm = g.tensor.matmul(T.psh[:, 0:TK], tile(T.ws, t, CUT), tile(T.xs, t, CUT), start=False, stop=(t == last))
-    mm.then_inc(s.sh, 1)
-    g.vector.wait_ge(s.sh, 1)
-    g.vector.tensor_scalar(T.h[:], T.psh[:, 0:TK], 0.0, None, AluOpType.max).then_inc(s.shr, 1)
+    pv, tt, tc, sv, vc = (T.pv0, T.pv1), (s.tt0, s.tt1), (s.tc0, s.tc1), (s.sv0, s.sv1), (s.vc0, s.vc1)
 
+    def copy(a, out, in_):
+        if a == 0:
+            return g.vector.tensor_copy(out, in_)
+        return g.scalar.activation(out, in_, ActivationFunctionType.Copy)
+
+    cq = (g.vector, g.scalar)
     g.tensor.wait_ge(s.si, n_si)
     g.tensor.wait_ge(s.lw, 16 * G)
     for a in range(G):
-        g.tensor.matmul(T.pst[:, a * TK:(a + 1) * TK], T.wq[:, a * TK:(a + 1) * TK], T.ident[:],
-                        start=True, stop=True).then_inc(s.tt, 1)
-    g.vector.wait_ge(s.tt, G)
-    g.vector.tensor_copy(T.wt[:], T.pst[:, 0:G * TK]).then_inc(s.tc, 1)
-    g.tensor.wait_ge(s.tc, 1)
-    g.tensor.wait_ge(s.shr, 1)
+        g.tensor.matmul(pv[a][:, 0:TK], T.wq[:, a * TK:(a + 1) * TK], T.ident[:], start=True, stop=True).then_inc(tt[a], 1)
+        cq[a].wait_ge(tt[a], 1)
+        copy(a, T.wt[:, a * TK:(a + 1) * TK], pv[a][:, 0:TK]).then_inc(tc[a], 1)
+    g.tensor.wait_ge(s.shr, G)
     for a in range(G):
-        g.tensor.matmul(T.psv[:, a * TK:(a + 1) * TK], T.wt[:, a * TK:(a + 1) * TK], T.h[:],
-                        start=True, stop=True).then_inc(s.sv, 1)
-    g.vector.wait_ge(s.sv, G)
-    g.vector.tensor_copy(T.v[:], T.psv[:, 0:G * TK]).then_inc(s.vc, 1)
+        g.tensor.wait_ge(tc[a], 1)
+        g.tensor.matmul(pv[a][:, TK:2 * TK], T.wt[:, a * TK:(a + 1) * TK], T.h[:], start=True, stop=True).then_inc(sv[a], 1)
+        cq[a].wait_ge(sv[a], 1)
+        copy(a, T.v[:, a * TK:(a + 1) * TK], pv[a][:, TK:2 * TK]).then_inc(vc[a], 1)
 
-    psy, sy = (T.psy0, T.psy1), (s.sy0, s.sy1)
-    g.tensor.wait_ge(s.zz, 2)
-    g.tensor.wait_ge(s.vc, 1)
+    psy = ((T.psqo, T.psy2), (T.psy0, T.psy1))
+    sy = ((s.sy00, s.sy01), (s.sy10, s.sy11))
+    ys, yr, st = (T.ys0, T.ys1), (s.yr0, s.yr1), (s.st0, s.st1)
+    g.tensor.wait_ge(s.sqo, 1)
     g.tensor.wait_ge(s.ae, n_in)
-    for i in range(2):
-        for a in range(G):
-            g.tensor.matmul(psy[i][:, 0:HF], T.z[:, PAD - a * WD:PAD - a * WD + TK],
-                            T.v[:, a * TK + i * HF:a * TK + (i + 1) * HF], start=(a == 0), stop=False)
-    g.tensor.wait_ge(s.al, n_in)
-    for i in range(2):
-        g.tensor.matmul(psy[i][:, 0:HF], T.nl[:], T.h[:, i * HF:(i + 1) * HF], start=False, stop=True).then_inc(sy[i], 1)
-    g.vector.wait_ge(sy[0], 1)
-    g.vector.tensor_copy(T.ys[:, 0:HF], psy[0][:, 0:HF]).then_inc(s.yr, 1)
-    g.scalar.wait_ge(sy[1], 1)
-    g.scalar.activation(T.ys[:, HF:TK], psy[1][:, 0:HF], ActivationFunctionType.Copy).then_inc(s.yr, 1)
-    g.sync.wait_ge(s.yr, 2)
-    g.sync.dma_start(T.y[:], T.ys[:]).then_inc(s.st, 16)
-    g.sync.wait_ge(s.st, 16)
+    for a in range(G):
+        g.tensor.wait_ge(vc[a], 1)
+        for i in range(2):
+            g.tensor.matmul(psy[a][i][0:HF, 0:HF], T.blk[:], T.v[:, a * TK + i * HF:a * TK + (i + 1) * HF],
+                            start=True, stop=False)
+    for a in range(G):
+        g.tensor.wait_ge(al_in[a], n_in)
+        for i in range(2):
+            g.tensor.matmul(psy[a][i][0:HF, 0:HF], half(T.nl, a), half(T.h, i), start=False, stop=True).then_inc(sy[a][i], 1)
+            cq[i].wait_ge(sy[a][i], 1)
+            copy(i, ys[a][0:HF, i * HF:(i + 1) * HF], psy[a][i][0:HF, 0:HF]).then_inc(yr[a], 1)
+        g.sync.wait_ge(yr[a], 2)
+        g.sync.dma_start(T.y[a * HF:(a + 1) * HF, :], ys[a][0:HF, :]).then_inc(st[a], 16)
+    for a in range(G):
+        g.sync.wait_ge(st[a], 16)
     g.wait_ge(s.snt, n_out)

from concourse.mybir import AluOpType, ActivationFunctionType

SIM_CORES = 256
TK = 128
KT = 4
CUT = 112
WD = (128 - CUT) * KT * TK // 128
G = TK // WD
HF = TK // 2
EB = G - 1
ENG_CHIP = 8
ENG_OUT = 8

SCRATCH = {
    "xs": ("sbuf", [128, KT * TK], "bfloat16"),
    "ws": ("sbuf", [128, KT * TK], "bfloat16"),
    "wq": ("sbuf", [128, G * TK], "bfloat16"),
    "xd": ("dram", [128, WD], "bfloat16"),
    "xt": ("sbuf", [128, KT * TK], "bfloat16"),
    "wl": ("sbuf", [128, KT * TK], "bfloat16"),
    "qo": ("sbuf", [128, TK], "float32"),
    "n1": ("sbuf", [128, TK], "bfloat16"),
    "hm": ("sbuf", [128, TK], "float32"),
    "h": ("sbuf", [128, TK], "bfloat16"),
    "ones": ("sbuf", [128, TK], "bfloat16"),
    "ident": ("sbuf", [128, TK], "bfloat16"),
    "wt": ("sbuf", [128, G * TK], "bfloat16"),
    "v": ("sbuf", [128, G * TK], "bfloat16"),
    "blk": ("sbuf", [128, WD], "bfloat16"),
    "nl": ("sbuf", [128, TK], "bfloat16"),
    "ys0": ("sbuf", [128, TK], "bfloat16"),
    "ys1": ("sbuf", [128, TK], "bfloat16"),
    "psqo": ("psum", [128, 512], "float32"),
    "psa0": ("psum", [128, 512], "float32"),
    "psa1": ("psum", [128, 512], "float32"),
    "pv0": ("psum", [128, 512], "float32"),
    "pv1": ("psum", [128, 512], "float32"),
    "psy0": ("psum", [128, 512], "float32"),
    "psy1": ("psum", [128, 512], "float32"),
    "psy2": ("psum", [128, 512], "float32"),
}
SEMAPHORES = ["le", "lq", "lx", "lw", "zq", "zo", "si", "so", "sqo", "sa0", "sa1", "sn0", "sn1", "sm0", "sm1", "shr",
              "tt0", "tt1", "tc0", "tc1", "sv0", "sv1", "vc0", "vc1", "ae", "al0", "al1",
              "sy00", "sy01", "sy10", "sy11", "yr0", "yr1", "st0", "st1", "snt"]


def _same_chip(topo, a, b):
    return topo.host(a) == topo.host(b) and topo.chip(a) == topo.chip(b)


def _engines(topo, src, dst):
    allowed = topo.mask(src, dst)
    bits = [b for b in range(allowed.bit_length()) if (allowed >> b) & 1]
    n = min(ENG_CHIP if _same_chip(topo, src, dst) else ENG_OUT, len(bits))
    m = 0
    for b in bits[::len(bits) // n][:n]:
        m |= 1 << b
    return m, n


def _way(topo, T, src, dst):
    if topo.may_write(src, dst):
        return src, [], dst
    c = [k for k in range(SIM_CORES)
         if k != src and T.rank_of(k) is None and _same_chip(topo, k, src) and topo.may_write(k, dst)]
    c.sort(key=lambda k: (topo.die(k) != topo.die(src), k))
    return src, c[:G], dst


def _send(g, T, topo, core, dst, out_ap, src_ap, sem):
    m, n = _engines(topo, core, dst)
    rid, pid = topo.addr(dst, core)
    g.remote_dma(out_ap, src_ap, sem, T.sem.snt, pid, rid, m)
    return n


def _identity(g, T, c0, c1):
    s = T.sem
    g.vector.memset(T.ones[:, c0:c1], 1.0).then_inc(s.zo, 1)
    g.wait_ge(s.zo, 1)
    g.affine_select(T.ident[:, c0:c1], T.ones[:, c0:c1], [[-1, c1 - c0]], AluOpType.is_equal, 0.0, -c0, 1).then_inc(s.si, 1)


def rank_program(g, core, T, topo):
    cores = list(T.cores)
    n_ranks = len(cores)
    ways = [_way(topo, T, cores[r], cores[(r + 1) % n_ranks]) for r in range(n_ranks)]
    rank = T.rank_of(core)
    s = T.sem
    al = (s.al0, s.al1)

    def half(buf, a):
        return buf[:, a * HF:(a + 1) * HF]

    if rank is None:
        for src, mid, dst in ways:
            if core in mid:
                a = mid.index(core)
                n_in = _engines(topo, src, core)[1]
                m, n = _engines(topo, core, dst)
                _identity(g, T, a * HF, (a + 1) * HF)
                g.wait_ge(s.si, 1)
                rid, pid = topo.addr(src, core)
                g.remote_dma(half(T.ident, a), half(T.ident, a), s.si, s.snt, pid, rid, m & topo.mask(core, src))
                if a == EB:
                    g.wait_ge(s.ae, n_in)
                    n += _send(g, T, topo, core, dst, T.blk[:], T.xd[:], s.ae)
                g.wait_ge(al[a], n_in)
                n += _send(g, T, topo, core, dst, half(T.nl, a), half(T.nl, a), al[a])
                g.wait_ge(s.snt, n)
        return

    def tile(buf, t, k):
        return buf[0:k, t * TK:(t + 1) * TK]

    last = KT - 1
    _, mid, nxt = ways[rank]
    psrc, pmid, _ = ways[(rank - 1) % n_ranks]
    n_in = _engines(topo, pmid[0] if pmid else psrc, core)[1]
    al_in = al if pmid else (s.al1, s.al1)
    rest = 128 - CUT
    n_si = sum(_engines(topo, k, nxt)[1] for k in mid) if mid else 1

    g.vector.memset(T.wq[:], 0.0).then_inc(s.zq, 1)
    g.sync.dma_start(T.xd[:], T.x[CUT:128, :]).then_inc(s.le, 16)
    g.scalar.dma_start(T.wl[0:rest, :], T.w[CUT:128, :]).then_inc(s.lq, 16)
    g.sync.dma_start(T.xt[0:rest, :], T.x[CUT:128, :]).then_inc(s.lq, 16)
    g.scalar.dma_start(T.ws[0:CUT, :], T.w[0:CUT, :]).then_inc(s.lx, 16)
    g.sync.dma_start(T.xs[0:CUT, :], T.x[0:CUT, :]).then_inc(s.lx, 16)
    for a, q in enumerate((g.sync, g.scalar)):
        q.wait_ge(s.zq, 1)
        q.dma_start(T.wq[a:128:G, a * TK:(a + 1) * TK], T.w[CUT:128, :]).then_inc(s.lw, 16)

    if not mid:
        _identity(g, T, 0, TK)
    g.wait_ge(s.le, 16)
    if mid:
        n_out = _send(g, T, topo, core, mid[EB], T.xd[:], T.xd[:], s.ae)
    else:
        n_out = _send(g, T, topo, core, nxt, T.blk[:], T.xd[:], s.ae)

    g.tensor.wait_ge(s.lq, 32)
    for t in range(KT):
        mm = g.tensor.matmul(T.psqo[:, 0:TK], tile(T.wl, t, rest), tile(T.xt, t, rest), start=(t == 0), stop=(t == last))
    mm.then_inc(s.so, 1)
    g.vector.wait_ge(s.so, 1)
    g.vector.tensor_scalar(T.qo[:], T.psqo[:, 0:TK], -1.0, None, AluOpType.mult).then_inc(s.sqo, 1)

    psa, sa, sn, sm = (T.psa0, T.psa1), (s.sa0, s.sa1), (s.sn0, s.sn1), (s.sm0, s.sm1)
    g.tensor.wait_ge(s.lx, 32)
    g.vector.wait_ge(s.sqo, 1)
    for a in range(G):
        for t in range(KT):
            mm = g.tensor.matmul(psa[a][:, 0:HF], tile(T.ws, t, CUT), T.xs[0:CUT, t * TK + a * HF:t * TK + (a + 1) * HF],
                                 start=(t == 0), stop=(t == last))
        mm.then_inc(sa[a], 1)
        g.vector.wait_ge(sa[a], 1)
        g.vector.tensor_tensor(half(T.n1, a), psa[a][:, 0:HF], half(T.qo, a), AluOpType.max).then_inc(sn[a], 1)
        g.vector.tensor_tensor(half(T.hm, a), psa[a][:, 0:HF], half(T.qo, a), AluOpType.subtract).then_inc(sm[a], 1)
        g.scalar.wait_ge(sm[a], 1)
        g.scalar.activation(half(T.h, a), half(T.hm, a), ActivationFunctionType.Relu).then_inc(s.shr, 1)
        g.wait_ge(sn[a], 1)
        if mid:
            n_out += _send(g, T, topo, core, mid[a], half(T.nl, a), half(T.n1, a), al[a])
    if not mid:
        n_out += _send(g, T, topo, core, nxt, T.nl[:], T.n1[:], s.al1)

    pv, tt, tc, sv, vc = (T.pv0, T.pv1), (s.tt0, s.tt1), (s.tc0, s.tc1), (s.sv0, s.sv1), (s.vc0, s.vc1)

    def copy(a, out, in_):
        if a == 0:
            return g.vector.tensor_copy(out, in_)
        return g.scalar.activation(out, in_, ActivationFunctionType.Copy)

    cq = (g.vector, g.scalar)
    g.tensor.wait_ge(s.si, n_si)
    g.tensor.wait_ge(s.lw, 16 * G)
    for a in range(G):
        g.tensor.matmul(pv[a][:, 0:TK], T.wq[:, a * TK:(a + 1) * TK], T.ident[:], start=True, stop=True).then_inc(tt[a], 1)
        cq[a].wait_ge(tt[a], 1)
        copy(a, T.wt[:, a * TK:(a + 1) * TK], pv[a][:, 0:TK]).then_inc(tc[a], 1)
    g.tensor.wait_ge(s.shr, G)
    for a in range(G):
        g.tensor.wait_ge(tc[a], 1)
        g.tensor.matmul(pv[a][:, TK:2 * TK], T.wt[:, a * TK:(a + 1) * TK], T.h[:], start=True, stop=True).then_inc(sv[a], 1)
        cq[a].wait_ge(sv[a], 1)
        copy(a, T.v[:, a * TK:(a + 1) * TK], pv[a][:, TK:2 * TK]).then_inc(vc[a], 1)

    psy = ((T.psqo, T.psy2), (T.psy0, T.psy1))
    sy = ((s.sy00, s.sy01), (s.sy10, s.sy11))
    ys, yr, st = (T.ys0, T.ys1), (s.yr0, s.yr1), (s.st0, s.st1)
    g.tensor.wait_ge(s.sqo, 1)
    g.tensor.wait_ge(s.ae, n_in)
    for a in range(G):
        g.tensor.wait_ge(vc[a], 1)
        for i in range(2):
            g.tensor.matmul(psy[a][i][0:HF, 0:HF], T.blk[:], T.v[:, a * TK + i * HF:a * TK + (i + 1) * HF],
                            start=True, stop=False)
    for a in range(G):
        g.tensor.wait_ge(al_in[a], n_in)
        for i in range(2):
            g.tensor.matmul(psy[a][i][0:HF, 0:HF], half(T.nl, a), half(T.h, i), start=False, stop=True).then_inc(sy[a][i], 1)
            cq[i].wait_ge(sy[a][i], 1)
            copy(i, ys[a][0:HF, i * HF:(i + 1) * HF], psy[a][i][0:HF, 0:HF]).then_inc(yr[a], 1)
        g.sync.wait_ge(yr[a], 2)
        g.sync.dma_start(T.y[a * HF:(a + 1) * HF, :], ys[a][0:HF, :]).then_inc(st[a], 16)
    for a in range(G):
        g.sync.wait_ge(st[a], 16)
    g.wait_ge(s.snt, n_out)
